import numpy as np
import ml_dtypes


def mxq(x, axis, fmt="e4m3"):
    dtype, down = {"e4m3": (ml_dtypes.float8_e4m3fn, 7), "e5m2": (ml_dtypes.float8_e5m2, 14)}[fmt]
    v = np.moveaxis(np.asarray(x, np.float32).astype(ml_dtypes.bfloat16).astype(np.float64), axis, -1)
    blocks = v.reshape(v.shape[:-1] + (-1, 32))
    amax = np.abs(blocks).max(-1, keepdims=True)
    byte = np.maximum(np.where(amax > 0, np.frexp(amax)[1] - 1 + 127, 0) - down, 1)
    scale = np.exp2(byte - 127.0)
    codes = (blocks / scale).astype(np.float32).astype(dtype).astype(np.float64)
    return np.moveaxis((codes * scale).reshape(v.shape), -1, axis)


WIDE = False


def mx_kscale(k):
    if not WIDE:
        return np.ones(k)
    levels = np.array([10, -10, 5, -5, 0])
    if k % 512:
        return np.exp2(np.random.permutation(np.resize(levels, k // 32))).repeat(32)
    a = np.empty((k // 512, 16))
    for p in range(k // 512):
        a[p, :8] = np.random.permutation(np.resize(levels, 8))
        for g in range(8):
            far = levels[np.abs(levels - a[p, g]) >= 10]
            a[p, g + 8] = far[np.random.randint(len(far))]
    return np.exp2(a.ravel()).repeat(32)


def f64(x):
    return np.asarray(x).astype(np.float64)


def striped8(idx):
    return np.concatenate([v.reshape(-1, 16).T for v in idx]).astype(np.uint16)


def unstriped8(offs):
    return np.stack([offs[16 * g:16 * g + 16].T.reshape(-1) for g in range(8)]).astype(np.int64)


E2M1 = np.array([0.0, 0.5, 1.0, 1.5, 2.0, 3.0, 4.0, 6.0, -0.0, -0.5, -1.0, -1.5, -2.0, -3.0, -4.0, -6.0])


def pack_weight(w, fmt):
    k, n = w.shape
    w = f64(np.asarray(w, np.float32).astype(ml_dtypes.bfloat16)).reshape(k // 32, 32, n)
    amax = np.abs(w).max(1)
    if fmt == "e4m3":
        byte = np.frexp(amax)[1] - 1 + 127 - 7
    else:
        mant, ex = np.frexp(amax / 6.0)
        byte = np.where(mant > 0.5, ex, ex - 1) + 127
    byte = np.clip(np.where(amax > 0, byte, 1), 1, 254)
    scaled = (w * np.exp2(127.0 - byte)[:, None, :]).reshape(k, n).astype(np.float32)
    by_word = np.ascontiguousarray(scaled.reshape(k // 512, 128, 4, n).transpose(0, 1, 3, 2))
    if fmt == "e4m3":
        words = by_word.astype(ml_dtypes.float8_e4m3fn).view(np.uint8)
    else:
        c = by_word.astype(ml_dtypes.float4_e2m1fn).view(np.uint8) & 0xF
        words = (c[..., 0::2] | (c[..., 1::2] << 4)).reshape(k // 512, 128, 2 * n)
    return np.ascontiguousarray(words), np.ascontiguousarray(byte.astype(np.uint8).reshape(k // 512, 16, n))


def unpack_weight(words, scales, fmt):
    g, _, n = scales.shape
    words = np.ascontiguousarray(words).reshape(g, 128, n, -1)
    if fmt == "e4m3":
        vals = words.view(ml_dtypes.float8_e4m3fn).astype(np.float64)
    else:
        nib = np.empty((g, 128, n, 4), np.uint8)
        nib[..., 0::2] = words & 0xF
        nib[..., 1::2] = words >> 4
        vals = E2M1[nib]
    vals = vals * np.repeat(np.exp2(scales.astype(np.float64) - 127.0), 8, axis=1)[..., None]
    return vals.transpose(0, 1, 3, 2).reshape(g * 512, n)


def gelu(v):
    return 0.5 * v * (1.0 + np.tanh(np.sqrt(2.0 / np.pi) * (v + 0.044715 * v**3)))


K, M, T, S = 1024, 1024, 1024, 512


def setup_inputs():
    n = np.random.standard_normal
    s = mx_kscale(K)[:, None]
    p_w = pack_weight(n((K, M)) / np.sqrt(K) / s, "e2m1")
    return {
        "xT": (n((K, T)) * s).astype(np.float32),
        "w_words": p_w[0],
        "w_scales": p_w[1],
        "wgt": np.repeat(np.random.uniform(0.5, 2.0, (8, S)), 16, axis=0).astype(np.float32),
        "b": (0.3 * n(1024)).astype(np.float32),
        "offs": striped8(np.stack([np.random.permutation(T)[:S] for _ in range(8)])),
    }


def reference(xT, w_words, w_scales, wgt, b, offs):
    idx = unstriped8(offs)
    group = np.arange(K) % 512 // 64
    xg = f64(wgt)[np.arange(K) // 4 % 128] * f64(xT)[np.arange(K)[:, None], idx[group]]
    xT_ = mxq(xg, 0, "e4m3")
    w_ = unpack_weight(w_words, w_scales, "e2m1")
    y = w_.T @ xT_
    return gelu(y + f64(b)[:, None])

@@ -1,0 +1,188 @@
+from contextlib import ExitStack
+
+import concourse.mybir as mybir
+from concourse.masks import make_identity
+
+K, N_OUT, T, S = 1024, 1024, 1024, 512
+FLOPS = 2 * K * N_OUT * S
+
+F32 = mybir.dt.float32
+BF16 = mybir.dt.bfloat16
+I32 = mybir.dt.int32
+U32 = mybir.dt.uint32
+U16 = mybir.dt.uint16
+U8 = mybir.dt.uint8
+FP8X4 = mybir.dt.float8_e4m3fn_x4
+FP4X4 = mybir.dt.float4_e2m1fn_x4
+MULT = mybir.AluOpType.mult
+GELU = mybir.ActivationFunctionType.Gelu_apprx_tanh
+
+P = 128
+PASSES = 2
+PACK = 4
+NT = N_OUT // P
+H = S // 2
+SPLIT = 4
+
+
+def tile_list_heads_gelu_kernel(tc, xT, w_words, w_scales, wgt, b, offs, out):
+    nc = tc.nc
+    with ExitStack() as ctx:
+        keep = ctx.enter_context(tc.tile_pool(name="keep", bufs=1))
+        psum = ctx.enter_context(tc.psum_pool(name="psum", bufs=1))
+
+        lists = keep.tile([P, S // 16], U16, name="lists")
+        wg = keep.tile([P, S], F32, name="wg")
+        planes = [keep.tile([P, T], F32, name=f"plane{i}") for i in range(PASSES * PACK)]
+        w_sb = keep.tile([P, PASSES, 2 * N_OUT], U8, name="w_sb", align_bytes=256)
+        ws_sb = keep.tile([P, PASSES, N_OUT], U8, name="ws_sb", align_bytes=256)
+        b_rows = keep.tile([P, P], F32, name="b_rows")
+        b_cols = keep.tile([P, NT], F32, name="b_cols")
+        ident = keep.tile([P, P], F32, name="ident")
+        warm = keep.tile([P, 1], F32, name="warm")
+        picked = [keep.tile([P, PACK, S], F32, name=f"picked{a}") for a in range(PASSES)]
+        grouped = [keep.tile([P, S, PACK], BF16, name=f"grouped{a}", align_bytes=256) for a in range(PASSES)]
+        codes = [keep.tile([P, S], U32, name=f"codes{a}", align_bytes=256) for a in range(PASSES)]
+        scales = [keep.tile([P, S], U8, name=f"scales{a}", align_bytes=256) for a in range(PASSES)]
+        result = keep.tile([P, NT, S], F32, name="result")
+        acc = [psum.tile([P, S], F32, name=f"acc{t}") for t in range(NT)]
+
+        x_view = xT.rearrange("(a p i) t -> a i p t", a=PASSES, i=PACK)
+
+        def load_plane(n):
+            nc.sync.dma_start(planes[n][:], x_view[n // PACK, n % PACK])
+
+        def load_w_scales(a):
+            for q in range(4):
+                nc.sync.dma_start(
+                    ws_sb[32 * q : 32 * q + 4, a, :].bitcast(I32), w_scales[a, 4 * q : 4 * q + 4, :].bitcast(I32)
+                )
+
+        w_view = w_words.rearrange("a p n -> p a n")
+
+        def load_w(a0, a1, t0, t1):
+            cols = slice(2 * P * t0, 2 * P * t1)
+            nc.sync.dma_start(w_sb[:, a0:a1, cols].bitcast(I32), w_view[:, a0:a1, cols].bitcast(I32))
+
+        nc.vector.memset(b_rows[:], 0.0)
+        nc.vector.memset(warm[:], 0.0)
+        nc.vector.memset(ws_sb[:].rearrange("p a n -> p (a n)").bitcast(I32), 0)
+        nc.scalar.dma_start(b_rows[0:NT, :], b.rearrange("(c p) -> c p", p=P))
+        nc.scalar.activation(warm[:], warm[:], GELU)
+        nc.sync.dma_start(lists[:], offs)
+        load_plane(0)
+        nc.sync.dma_start(wg[:, 0:H], wgt[:, 0:H])
+        nc.sync.dma_start(wg[:, H:S], wgt[:, H:S])
+        for n in range(1, 6):
+            load_plane(n)
+        load_w_scales(0)
+        load_w(0, 1, SPLIT, NT)
+        for n in range(6, 8):
+            load_plane(n)
+        load_w(0, 1, 0, SPLIT)
+        load_w_scales(1)
+        load_w(1, 2, 0, SPLIT)
+        load_w(1, 2, SPLIT, NT)
+
+        make_identity(nc, ident[:])
+        nc.tensor.transpose(acc[NT - 1][:, 0:P], b_rows[:], ident[:])
+        nc.scalar.copy(b_cols[:], acc[NT - 1][:, 0:NT])
+
+        def gather(n, c0, cn):
+            nc.vector.tensor_tensor(
+                picked[n // PACK][:, n % PACK, c0 : c0 + cn],
+                planes[n][:].indirect(lists[:, c0 // 16 : (c0 + cn) // 16]),
+                wg[:, c0 : c0 + cn],
+                MULT,
+            )
+
+        def interleave(eng, a, c0, cn, i0=0, i1=PACK):
+            dst = grouped[a][:, c0 : c0 + cn, i0:i1].rearrange("p (c j) i -> p c i j", j=4)
+            src = picked[a][:, i0:i1, c0 : c0 + cn].rearrange("p i (c j) -> p c i j", j=4)
+            if eng == "v":
+                nc.vector.tensor_copy(dst, src)
+            else:
+                nc.scalar.copy(dst, src)
+
+        def quantize(a, c0, cn):
+            nc.vector.quantize_mx(
+                out=codes[a][:, c0 : c0 + cn].bitcast(FP8X4),
+                scales=scales[a][:, c0 : c0 + cn],
+                in_=grouped[a][:, c0 : c0 + cn, :].rearrange("p c i -> p (c i)"),
+            )
+
+        def multiply(a, t, c0, cn):
+            nc.tensor.matmul_mx(
+                out=acc[t][:, c0 : c0 + cn],
+                lhsT=w_sb[:, a, 2 * P * t : 2 * P * (t + 1)].bitcast(FP4X4),
+                lhsT_scale=ws_sb[:, a, P * t : P * (t + 1)],
+                rhs=codes[a][:, c0 : c0 + cn].bitcast(FP8X4),
+                rhs_scale=scales[a][:, c0 : c0 + cn],
+                start=(a == 0),
+                stop=(a == PASSES - 1),
+            )
+
+        out_view = out.rearrange("(t p) j -> p t j", p=P)
+
+        def finish(t, c0, cn):
+            nc.scalar.activation(result[:, t, c0 : c0 + cn], acc[t][:, c0 : c0 + cn], GELU, bias=b_cols[:, t : t + 1])
+
+        def store(t0, tn, c0, cn):
+            nc.sync.dma_start(out_view[:, t0 : t0 + tn, c0 : c0 + cn], result[:, t0 : t0 + tn, c0 : c0 + cn])
+
+        for n in range(4):
+            gather(n, 0, H)
+            gather(n, H, H)
+        interleave("s", 0, 0, H)
+        interleave("s", 0, H, H)
+        gather(4, 0, H)
+        gather(4, H, H)
+        gather(5, 0, H)
+        interleave("s", 1, 0, H, 0, 2)
+        gather(5, H, H)
+        interleave("s", 1, H, H, 0, 2)
+        quantize(0, 0, S)
+        gather(6, 0, H)
+        gather(6, H, H)
+        whole = range(SPLIT, NT)
+        halved = range(SPLIT)
+        for t in whole:
+            multiply(0, t, 0, S)
+        for q in range(2):
+            gather(7, 128 * q, 128)
+        for q in range(2):
+            interleave("v", 1, 128 * q, 128, 2, 4)
+        for q in range(2):
+            quantize(1, 128 * q, 128)
+        for q in range(2, 4):
+            gather(7, 128 * q, 128)
+        for q in range(2, 4):
+            interleave("v", 1, 128 * q, 128, 2, 4)
+        for q in range(2, 4):
+            quantize(1, 128 * q, 128)
+        for t in halved:
+            multiply(0, t, 0, 128)
+        for t in halved:
+            multiply(1, t, 0, 128)
+            multiply(0, t, 128, 128)
+            multiply(1, t, 128, 128)
+            finish(t, 0, H)
+            if t < 2:
+                store(t, 1, 0, H)
+            elif t == 3:
+                store(t - 1, 2, 0, H)
+        for t in whole:
+            multiply(1, t, 0, S)
+            finish(t, 0, S)
+            store(t, 1, 0, S)
+        for t in halved:
+            for q in range(2, 4):
+                multiply(0, t, 128 * q, 128)
+                multiply(1, t, 128 * q, 128)
+            finish(t, H, H)
+            if t == 1:
+                store(t - 1, 2, H, H)
+            elif t == 2:
+                store(t, 1, H, H)
+            elif t == 3:
+                nc.scalar.dma_start(out_view[:, t, H:S], result[:, t, H:S])

@@ -22,7 +22,8 @@ PASSES = 2
 PACK = 4
 NT = N_OUT // P
 H = S // 2
-SPLIT = 4
+Q = S // 4
+SPLIT = 6
 
 
 def tile_list_heads_gelu_kernel(tc, xT, w_words, w_scales, wgt, b, offs, out):
@@ -40,12 +41,14 @@ def tile_list_heads_gelu_kernel(tc, xT, w_words, w_scales, wgt, b, offs, out):
         b_cols = keep.tile([P, NT], F32, name="b_cols")
         ident = keep.tile([P, P], F32, name="ident")
         warm = keep.tile([P, 1], F32, name="warm")
-        picked = [keep.tile([P, PACK, S], F32, name=f"picked{a}") for a in range(PASSES)]
+        picked0 = keep.tile([P, PACK, S], F32, name="picked0")
+        picked1 = keep.tile([P, 7, H], F32, name="picked1")
         grouped = [keep.tile([P, S, PACK], BF16, name=f"grouped{a}", align_bytes=256) for a in range(PASSES)]
         codes = [keep.tile([P, S], U32, name=f"codes{a}", align_bytes=256) for a in range(PASSES)]
         scales = [keep.tile([P, S], U8, name=f"scales{a}", align_bytes=256) for a in range(PASSES)]
         result = keep.tile([P, NT, S], F32, name="result")
-        acc = [psum.tile([P, S], F32, name=f"acc{t}") for t in range(NT)]
+        halves = [[psum.tile([P, 2, H], F32, name=f"half{h}{u}") for u in range(SPLIT // 2)] for h in range(2)]
+        acc = {t: psum.tile([P, S], F32, name=f"acc{t}") for t in range(SPLIT, NT)}
 
         x_view = xT.rearrange("(a p i) t -> a i p t", a=PASSES, i=PACK)
 
@@ -73,36 +76,31 @@ def tile_list_heads_gelu_kernel(tc, xT, w_words, w_scales, wgt, b, offs, out):
         load_plane(0)
         nc.sync.dma_start(wg[:, 0:H], wgt[:, 0:H])
         nc.sync.dma_start(wg[:, H:S], wgt[:, H:S])
-        for n in range(1, 6):
+        for n in range(1, 5):
             load_plane(n)
         load_w_scales(0)
-        load_w(0, 1, SPLIT, NT)
-        for n in range(6, 8):
+        load_w(0, 1, 0, NT)
+        for n in range(5, 8):
             load_plane(n)
-        load_w(0, 1, 0, SPLIT)
         load_w_scales(1)
-        load_w(1, 2, 0, SPLIT)
-        load_w(1, 2, SPLIT, NT)
+        load_w(1, 2, 0, NT // 2)
+        load_w(1, 2, NT // 2, NT)
 
         make_identity(nc, ident[:])
         nc.tensor.transpose(acc[NT - 1][:, 0:P], b_rows[:], ident[:])
         nc.scalar.copy(b_cols[:], acc[NT - 1][:, 0:NT])
 
-        def gather(n, c0, cn):
+        def gather(n, dst, c0, cn):
             nc.vector.tensor_tensor(
-                picked[n // PACK][:, n % PACK, c0 : c0 + cn],
+                dst,
                 planes[n][:].indirect(lists[:, c0 // 16 : (c0 + cn) // 16]),
                 wg[:, c0 : c0 + cn],
                 MULT,
             )
 
-        def interleave(eng, a, c0, cn, i0=0, i1=PACK):
+        def interleave(copy, a, src, c0, cn, i0, i1):
             dst = grouped[a][:, c0 : c0 + cn, i0:i1].rearrange("p (c j) i -> p c i j", j=4)
-            src = picked[a][:, i0:i1, c0 : c0 + cn].rearrange("p i (c j) -> p c i j", j=4)
-            if eng == "v":
-                nc.vector.tensor_copy(dst, src)
-            else:
-                nc.scalar.copy(dst, src)
+            copy(dst, src.rearrange("p i (c j) -> p c i j", j=4))
 
         def quantize(a, c0, cn):
             nc.vector.quantize_mx(
@@ -111,78 +109,93 @@ def tile_list_heads_gelu_kernel(tc, xT, w_words, w_scales, wgt, b, offs, out):
                 in_=grouped[a][:, c0 : c0 + cn, :].rearrange("p c i -> p (c i)"),
             )
 
-        def multiply(a, t, c0, cn):
+        def multiply(dst, a, t, c0, cn, start, stop):
             nc.tensor.matmul_mx(
-                out=acc[t][:, c0 : c0 + cn],
+                out=dst,
                 lhsT=w_sb[:, a, 2 * P * t : 2 * P * (t + 1)].bitcast(FP4X4),
                 lhsT_scale=ws_sb[:, a, P * t : P * (t + 1)],
                 rhs=codes[a][:, c0 : c0 + cn].bitcast(FP8X4),
                 rhs_scale=scales[a][:, c0 : c0 + cn],
-                start=(a == 0),
-                stop=(a == PASSES - 1),
+                start=start,
+                stop=stop,
             )
+
+        def multiply_whole(a, t):
+            multiply(acc[t][:], a, t, 0, S, a == 0, a == PASSES - 1)
+
+        def multiply_half(a, h, u, opens, closes):
+            for q in range(2):
+                for s in range(2):
+                    first = opens and q == 0 and s == 0
+                    last = closes and q == 1 and s == 1
+                    multiply(halves[h][u][:, s, q * Q : (q + 1) * Q], a, 2 * u + s, h * H + q * Q, Q, first, last)
 
         out_view = out.rearrange("(t p) j -> p t j", p=P)
 
-        def finish(t, c0, cn):
-            nc.scalar.activation(result[:, t, c0 : c0 + cn], acc[t][:, c0 : c0 + cn], GELU, bias=b_cols[:, t : t + 1])
+        def finish(src, t, c0, cn):
+            nc.scalar.activation(result[:, t, c0 : c0 + cn], src, GELU, bias=b_cols[:, t : t + 1])
 
         def store(t0, tn, c0, cn):
             nc.sync.dma_start(out_view[:, t0 : t0 + tn, c0 : c0 + cn], result[:, t0 : t0 + tn, c0 : c0 + cn])
 
-        for n in range(4):
-            gather(n, 0, H)
-            gather(n, H, H)
-        interleave("s", 0, 0, H)
-        interleave("s", 0, H, H)
-        gather(4, 0, H)
-        gather(4, H, H)
-        gather(5, 0, H)
-        interleave("s", 1, 0, H, 0, 2)
-        gather(5, H, H)
-        interleave("s", 1, H, H, 0, 2)
+        on_scalar, on_vector = nc.scalar.copy, nc.vector.tensor_copy
+        pairs = SPLIT // 2
+
+        gather(0, picked0[:, 0, 0:H], 0, H)
+        gather(0, picked0[:, 0, H:S], H, H)
+        gather(1, picked0[:, 1, :], 0, S)
+        interleave(on_scalar, 0, picked0[:, 0:2, :], 0, S, 0, 2)
+        gather(2, picked0[:, 2, :], 0, S)
+        for h in range(2):
+            gather(3, picked0[:, 3, h * H : (h + 1) * H], h * H, H)
+            interleave(on_scalar, 0, picked0[:, 2:4, h * H : (h + 1) * H], h * H, H, 2, 4)
+        gather(4, picked1[:, 5, :], 0, H)
+        gather(4, picked1[:, 1, :], H, H)
+        gather(5, picked1[:, 6, :], 0, H)
+        interleave(on_scalar, 1, picked1[:, 5:7, :], 0, H, 0, 2)
         quantize(0, 0, S)
-        gather(6, 0, H)
-        gather(6, H, H)
+        gather(6, picked1[:, 2, :], 0, H)
         whole = range(SPLIT, NT)
-        halved = range(SPLIT)
         for t in whole:
-            multiply(0, t, 0, S)
+            multiply_whole(0, t)
+        for u in range(pairs):
+            multiply_half(0, 0, u, True, False)
+        multiply_half(0, 1, pairs - 1, True, False)
         for q in range(2):
-            gather(7, 128 * q, 128)
+            gather(7, picked1[:, 3, q * Q : (q + 1) * Q], q * Q, Q)
+            interleave(on_scalar, 1, picked1[:, 2:4, q * Q : (q + 1) * Q], q * Q, Q, 2, 4)
+        gather(7, picked1[:, 4, :], H, H)
         for q in range(2):
-            interleave("v", 1, 128 * q, 128, 2, 4)
+            quantize(1, q * Q, Q)
+        gather(5, picked1[:, 2, :], H, H)
         for q in range(2):
-            quantize(1, 128 * q, 128)
-        for q in range(2, 4):
-            gather(7, 128 * q, 128)
-        for q in range(2, 4):
-            interleave("v", 1, 128 * q, 128, 2, 4)
-        for q in range(2, 4):
-            quantize(1, 128 * q, 128)
-        for t in halved:
-            multiply(0, t, 0, 128)
-        for t in halved:
-            multiply(1, t, 0, 128)
-            multiply(0, t, 128, 128)
-            multiply(1, t, 128, 128)
-            finish(t, 0, H)
-            if t < 2:
-                store(t, 1, 0, H)
-            elif t == 3:
-                store(t - 1, 2, 0, H)
+            gather(6, picked1[:, 3, q * Q : (q + 1) * Q], H + q * Q, Q)
+        for q in range(2):
+            interleave(on_vector, 1, picked1[:, 1:5, q * Q : (q + 1) * Q], H + q * Q, Q, 0, 4)
+        for q in range(2):
+            quantize(1, H + q * Q, Q)
+
+        for u in range(pairs):
+            multiply_half(1, 0, u, False, True)
+            for s in range(2):
+                finish(halves[0][u][:, s, :], 2 * u + s, 0, H)
+                if u == 0:
+                    store(s, 1, 0, H)
+            if u > 0:
+                store(2 * u, 2, 0, H)
         for t in whole:
-            multiply(1, t, 0, S)
-            finish(t, 0, S)
+            multiply_whole(1, t)
+            finish(acc[t][:], t, 0, S)
             store(t, 1, 0, S)
-        for t in halved:
-            for q in range(2, 4):
-                multiply(0, t, 128 * q, 128)
-                multiply(1, t, 128 * q, 128)
-            finish(t, H, H)
-            if t == 1:
-                store(t - 1, 2, H, H)
-            elif t == 2:
-                store(t, 1, H, H)
-            elif t == 3:
-                nc.scalar.dma_start(out_view[:, t, H:S], result[:, t, H:S])
+        for u in range(pairs - 1):
+            multiply_half(1, 1, u, True, False)
+            multiply_half(0, 1, u, False, True)
+            for s in range(2):
+                finish(halves[1][u][:, s, :], 2 * u + s, H, H)
+            store(2 * u, 2, H, H)
+        u = pairs - 1
+        multiply_half(1, 1, u, False, True)
+        finish(halves[1][u][:, 0, :], 2 * u, H, H)
+        store(2 * u, 1, H, H)
+        finish(halves[1][u][:, 1, :], 2 * u + 1, H, H)
+        nc.scalar.dma_start(out_view[:, 2 * u + 1, H:S], result[:, 2 * u + 1, H:S])

@@ -74,14 +74,15 @@ def tile_list_heads_gelu_kernel(tc, xT, w_words, w_scales, wgt, b, offs, out):
         nc.scalar.activation(warm[:], warm[:], GELU)
         nc.sync.dma_start(lists[:], offs)
         load_plane(0)
-        nc.sync.dma_start(wg[:, 0:H], wgt[:, 0:H])
-        nc.sync.dma_start(wg[:, H:S], wgt[:, H:S])
+        nc.sync.dma_start(wg[:, 0:Q], wgt[:, 0:Q])
+        nc.sync.dma_start(wg[:, Q:S], wgt[:, Q:S])
         for n in range(1, 5):
             load_plane(n)
         load_w_scales(0)
-        load_w(0, 1, 0, NT)
+        load_w(0, 1, 0, SPLIT)
         for n in range(5, 8):
             load_plane(n)
+        load_w(0, 1, SPLIT, NT)
         load_w_scales(1)
         load_w(1, 2, 0, NT // 2)
         load_w(1, 2, NT // 2, NT)
@@ -123,11 +124,11 @@ def tile_list_heads_gelu_kernel(tc, xT, w_words, w_scales, wgt, b, offs, out):
         def multiply_whole(a, t):
             multiply(acc[t][:], a, t, 0, S, a == 0, a == PASSES - 1)
 
-        def multiply_half(a, h, u, opens, closes):
+        def multiply_half(a, h, u):
             for q in range(2):
                 for s in range(2):
-                    first = opens and q == 0 and s == 0
-                    last = closes and q == 1 and s == 1
+                    first = a == 0 and q == 0 and s == 0
+                    last = a == PASSES - 1 and q == 1 and s == 1
                     multiply(halves[h][u][:, s, q * Q : (q + 1) * Q], a, 2 * u + s, h * H + q * Q, Q, first, last)
 
         out_view = out.rearrange("(t p) j -> p t j", p=P)
@@ -141,8 +142,8 @@ def tile_list_heads_gelu_kernel(tc, xT, w_words, w_scales, wgt, b, offs, out):
         on_scalar, on_vector = nc.scalar.copy, nc.vector.tensor_copy
         pairs = SPLIT // 2
 
-        gather(0, picked0[:, 0, 0:H], 0, H)
-        gather(0, picked0[:, 0, H:S], H, H)
+        gather(0, picked0[:, 0, 0:Q], 0, Q)
+        gather(0, picked0[:, 0, Q:S], Q, S - Q)
         gather(1, picked0[:, 1, :], 0, S)
         interleave(on_scalar, 0, picked0[:, 0:2, :], 0, S, 0, 2)
         gather(2, picked0[:, 2, :], 0, S)
@@ -150,17 +151,18 @@ def tile_list_heads_gelu_kernel(tc, xT, w_words, w_scales, wgt, b, offs, out):
             gather(3, picked0[:, 3, h * H : (h + 1) * H], h * H, H)
             interleave(on_scalar, 0, picked0[:, 2:4, h * H : (h + 1) * H], h * H, H, 2, 4)
         gather(4, picked1[:, 5, :], 0, H)
+        quantize(0, 0, H)
         gather(4, picked1[:, 1, :], H, H)
+        quantize(0, H, H)
         gather(5, picked1[:, 6, :], 0, H)
         interleave(on_scalar, 1, picked1[:, 5:7, :], 0, H, 0, 2)
-        quantize(0, 0, S)
         gather(6, picked1[:, 2, :], 0, H)
         whole = range(SPLIT, NT)
+        for h in range(2):
+            for u in range(pairs):
+                multiply_half(0, h, u)
         for t in whole:
             multiply_whole(0, t)
-        for u in range(pairs):
-            multiply_half(0, 0, u, True, False)
-        multiply_half(0, 1, pairs - 1, True, False)
         for q in range(2):
             gather(7, picked1[:, 3, q * Q : (q + 1) * Q], q * Q, Q)
             interleave(on_scalar, 1, picked1[:, 2:4, q * Q : (q + 1) * Q], q * Q, Q, 2, 4)
@@ -176,7 +178,7 @@ def tile_list_heads_gelu_kernel(tc, xT, w_words, w_scales, wgt, b, offs, out):
             quantize(1, H + q * Q, Q)
 
         for u in range(pairs):
-            multiply_half(1, 0, u, False, True)
+            multiply_half(1, 0, u)
             for s in range(2):
                 finish(halves[0][u][:, s, :], 2 * u + s, 0, H)
                 if u == 0:
@@ -188,13 +190,12 @@ def tile_list_heads_gelu_kernel(tc, xT, w_words, w_scales, wgt, b, offs, out):
             finish(acc[t][:], t, 0, S)
             store(t, 1, 0, S)
         for u in range(pairs - 1):
-            multiply_half(1, 1, u, True, False)
-            multiply_half(0, 1, u, False, True)
+            multiply_half(1, 1, u)
             for s in range(2):
                 finish(halves[1][u][:, s, :], 2 * u + s, H, H)
             store(2 * u, 2, H, H)
         u = pairs - 1
-        multiply_half(1, 1, u, False, True)
+        multiply_half(1, 1, u)
         finish(halves[1][u][:, 0, :], 2 * u, H, H)
         store(2 * u, 1, H, H)
         finish(halves[1][u][:, 1, :], 2 * u + 1, H, H)

@@ -72,17 +72,17 @@ def tile_list_heads_gelu_kernel(tc, xT, w_words, w_scales, wgt, b, offs, out):
         nc.vector.memset(ws_sb[:].rearrange("p a n -> p (a n)").bitcast(I32), 0)
         nc.scalar.dma_start(b_rows[0:NT, :], b.rearrange("(c p) -> c p", p=P))
         nc.scalar.activation(warm[:], warm[:], GELU)
-        nc.sync.dma_start(lists[:], offs)
         load_plane(0)
+        nc.sync.dma_start(lists[:], offs)
         nc.sync.dma_start(wg[:, 0:Q], wgt[:, 0:Q])
         nc.sync.dma_start(wg[:, Q:S], wgt[:, Q:S])
         for n in range(1, 5):
             load_plane(n)
         load_w_scales(0)
-        load_w(0, 1, 0, SPLIT)
+        load_w(0, 1, 0, 4)
         for n in range(5, 8):
             load_plane(n)
-        load_w(0, 1, SPLIT, NT)
+        load_w(0, 1, 4, NT)
         load_w_scales(1)
         load_w(1, 2, 0, NT // 2)
         load_w(1, 2, NT // 2, NT)
@@ -124,11 +124,11 @@ def tile_list_heads_gelu_kernel(tc, xT, w_words, w_scales, wgt, b, offs, out):
         def multiply_whole(a, t):
             multiply(acc[t][:], a, t, 0, S, a == 0, a == PASSES - 1)
 
-        def multiply_half(a, h, u):
+        def multiply_half(a, h, u, opens=0):
             for q in range(2):
                 for s in range(2):
-                    first = a == 0 and q == 0 and s == 0
-                    last = a == PASSES - 1 and q == 1 and s == 1
+                    first = a == opens and q == 0 and s == 0
+                    last = a != opens and q == 1 and s == 1
                     multiply(halves[h][u][:, s, q * Q : (q + 1) * Q], a, 2 * u + s, h * H + q * Q, Q, first, last)
 
         out_view = out.rearrange("(t p) j -> p t j", p=P)
@@ -159,8 +159,9 @@ def tile_list_heads_gelu_kernel(tc, xT, w_words, w_scales, wgt, b, offs, out):
         gather(6, picked1[:, 2, :], 0, H)
         whole = range(SPLIT, NT)
         for h in range(2):
-            for u in range(pairs):
+            for u in range(pairs - 1):
                 multiply_half(0, h, u)
+        multiply_half(0, 0, pairs - 1)
         for t in whole:
             multiply_whole(0, t)
         for q in range(2):
@@ -195,7 +196,8 @@ def tile_list_heads_gelu_kernel(tc, xT, w_words, w_scales, wgt, b, offs, out):
                 finish(halves[1][u][:, s, :], 2 * u + s, H, H)
             store(2 * u, 2, H, H)
         u = pairs - 1
-        multiply_half(1, 1, u)
+        multiply_half(1, 1, u, opens=1)
+        multiply_half(0, 1, u, opens=1)
         finish(halves[1][u][:, 0, :], 2 * u, H, H)
         store(2 * u, 1, H, H)
         finish(halves[1][u][:, 1, :], 2 * u + 1, H, H)

@@ -23,6 +23,7 @@ PACK = 4
 NT = N_OUT // P
 H = S // 2
 Q = S // 4
+FOUR = 4
 SPLIT = 6
 
 
@@ -42,12 +43,14 @@ def tile_list_heads_gelu_kernel(tc, xT, w_words, w_scales, wgt, b, offs, out):
         ident = keep.tile([P, P], F32, name="ident")
         warm = keep.tile([P, 1], F32, name="warm")
         picked0 = keep.tile([P, PACK, S], F32, name="picked0")
-        picked1 = keep.tile([P, 7, H], F32, name="picked1")
+        picked45 = keep.tile([P, 2, S], F32, name="picked45")
+        picked67 = keep.tile([P, 3, H], F32, name="picked67")
         grouped = [keep.tile([P, S, PACK], BF16, name=f"grouped{a}", align_bytes=256) for a in range(PASSES)]
         codes = [keep.tile([P, S], U32, name=f"codes{a}", align_bytes=256) for a in range(PASSES)]
         scales = [keep.tile([P, S], U8, name=f"scales{a}", align_bytes=256) for a in range(PASSES)]
         result = keep.tile([P, NT, S], F32, name="result")
-        halves = [[psum.tile([P, 2, H], F32, name=f"half{h}{u}") for u in range(SPLIT // 2)] for h in range(2)]
+        quarters = [psum.tile([P, FOUR, Q], F32, name=f"quarter{q}") for q in range(2)]
+        halves = [{2: psum.tile([P, 2, H], F32, name="half02")}, {u: psum.tile([P, 2, H], F32, name=f"half1{u}") for u in range(3)}]
         acc = {t: psum.tile([P, S], F32, name=f"acc{t}") for t in range(SPLIT, NT)}
 
         x_view = xT.rearrange("(a p i) t -> a i p t", a=PASSES, i=PACK)
@@ -82,10 +85,10 @@ def tile_list_heads_gelu_kernel(tc, xT, w_words, w_scales, wgt, b, offs, out):
         load_w(0, 1, 0, 4)
         for n in range(5, 8):
             load_plane(n)
-        load_w(0, 1, 4, NT)
+        load_w(0, 1, FOUR, NT)
         load_w_scales(1)
-        load_w(1, 2, 0, NT // 2)
-        load_w(1, 2, NT // 2, NT)
+        load_w(1, 2, 0, FOUR)
+        load_w(1, 2, FOUR, NT)
 
         make_identity(nc, ident[:])
         nc.tensor.transpose(acc[NT - 1][:, 0:P], b_rows[:], ident[:])
@@ -131,6 +134,10 @@ def tile_list_heads_gelu_kernel(tc, xT, w_words, w_scales, wgt, b, offs, out):
                     last = a != opens and q == 1 and s == 1
                     multiply(halves[h][u][:, s, q * Q : (q + 1) * Q], a, 2 * u + s, h * H + q * Q, Q, first, last)
 
+        def multiply_quarter(a, q):
+            for t in range(FOUR):
+                multiply(quarters[q][:, t, :], a, t, q * Q, Q, a == 0 and t == 0, a == 1 and t == FOUR - 1)
+
         out_view = out.rearrange("(t p) j -> p t j", p=P)
 
         def finish(src, t, c0, cn):
@@ -150,42 +157,47 @@ def tile_list_heads_gelu_kernel(tc, xT, w_words, w_scales, wgt, b, offs, out):
         for h in range(2):
             gather(3, picked0[:, 3, h * H : (h + 1) * H], h * H, H)
             interleave(on_scalar, 0, picked0[:, 2:4, h * H : (h + 1) * H], h * H, H, 2, 4)
-        gather(4, picked1[:, 5, :], 0, H)
+        gather(4, picked45[:, 0, 0:H], 0, H)
         quantize(0, 0, H)
-        gather(4, picked1[:, 1, :], H, H)
+        gather(4, picked45[:, 0, H:S], H, H)
         quantize(0, H, H)
-        gather(5, picked1[:, 6, :], 0, H)
-        interleave(on_scalar, 1, picked1[:, 5:7, :], 0, H, 0, 2)
-        gather(6, picked1[:, 2, :], 0, H)
-        whole = range(SPLIT, NT)
         for h in range(2):
-            for u in range(pairs - 1):
-                multiply_half(0, h, u)
+            gather(5, picked45[:, 1, h * H : (h + 1) * H], h * H, H)
+            interleave(on_scalar, 1, picked45[:, :, h * H : (h + 1) * H], h * H, H, 0, 2)
+        gather(6, picked67[:, 0, :], 0, H)
+        whole = range(SPLIT, NT)
+        for q in range(2):
+            multiply_quarter(0, q)
+        for u in range(pairs - 1):
+            multiply_half(0, 1, u)
         multiply_half(0, 0, pairs - 1)
         for t in whole:
             multiply_whole(0, t)
         for q in range(2):
-            gather(7, picked1[:, 3, q * Q : (q + 1) * Q], q * Q, Q)
-            interleave(on_scalar, 1, picked1[:, 2:4, q * Q : (q + 1) * Q], q * Q, Q, 2, 4)
-        gather(7, picked1[:, 4, :], H, H)
+            gather(7, picked67[:, 1, q * Q : (q + 1) * Q], q * Q, Q)
+            interleave(on_scalar, 1, picked67[:, 0:2, q * Q : (q + 1) * Q], q * Q, Q, 2, 4)
+        gather(7, picked67[:, 2, :], H, H)
         for q in range(2):
             quantize(1, q * Q, Q)
-        gather(5, picked1[:, 2, :], H, H)
         for q in range(2):
-            gather(6, picked1[:, 3, q * Q : (q + 1) * Q], H + q * Q, Q)
+            gather(6, picked67[:, 1, q * Q : (q + 1) * Q], H + q * Q, Q)
         for q in range(2):
-            interleave(on_vector, 1, picked1[:, 1:5, q * Q : (q + 1) * Q], H + q * Q, Q, 0, 4)
+            interleave(on_vector, 1, picked67[:, 1:3, q * Q : (q + 1) * Q], H + q * Q, Q, 2, 4)
         for q in range(2):
             quantize(1, H + q * Q, Q)
 
-        for u in range(pairs):
-            multiply_half(1, 0, u)
-            for s in range(2):
-                finish(halves[0][u][:, s, :], 2 * u + s, 0, H)
-                if u == 0:
-                    store(s, 1, 0, H)
-            if u > 0:
-                store(2 * u, 2, 0, H)
+        for q in range(2):
+            multiply_quarter(1, q)
+            for t in range(FOUR):
+                finish(quarters[q][:, t, :], t, q * Q, Q)
+                if q == 1 and t < 2:
+                    store(t, 1, 0, H)
+        store(2, 2, 0, H)
+        u = pairs - 1
+        multiply_half(1, 0, u)
+        for s in range(2):
+            finish(halves[0][u][:, s, :], 2 * u + s, 0, H)
+        store(2 * u, 2, 0, H)
         for t in whole:
             multiply_whole(1, t)
             finish(acc[t][:], t, 0, S)

@@ -43,8 +43,7 @@ def tile_list_heads_gelu_kernel(tc, xT, w_words, w_scales, wgt, b, offs, out):
         ident = keep.tile([P, P], F32, name="ident")
         warm = keep.tile([P, 1], F32, name="warm")
         picked0 = keep.tile([P, PACK, S], F32, name="picked0")
-        picked45 = keep.tile([P, 2, S], F32, name="picked45")
-        picked67 = keep.tile([P, 3, H], F32, name="picked67")
+        picked1 = keep.tile([P, 7, H], F32, name="picked1")
         grouped = [keep.tile([P, S, PACK], BF16, name=f"grouped{a}", align_bytes=256) for a in range(PASSES)]
         codes = [keep.tile([P, S], U32, name=f"codes{a}", align_bytes=256) for a in range(PASSES)]
         scales = [keep.tile([P, S], U8, name=f"scales{a}", align_bytes=256) for a in range(PASSES)]
@@ -157,14 +156,13 @@ def tile_list_heads_gelu_kernel(tc, xT, w_words, w_scales, wgt, b, offs, out):
         for h in range(2):
             gather(3, picked0[:, 3, h * H : (h + 1) * H], h * H, H)
             interleave(on_scalar, 0, picked0[:, 2:4, h * H : (h + 1) * H], h * H, H, 2, 4)
-        gather(4, picked45[:, 0, 0:H], 0, H)
+        gather(4, picked1[:, 5, :], 0, H)
         quantize(0, 0, H)
-        gather(4, picked45[:, 0, H:S], H, H)
+        gather(4, picked1[:, 1, :], H, H)
         quantize(0, H, H)
-        for h in range(2):
-            gather(5, picked45[:, 1, h * H : (h + 1) * H], h * H, H)
-            interleave(on_scalar, 1, picked45[:, :, h * H : (h + 1) * H], h * H, H, 0, 2)
-        gather(6, picked67[:, 0, :], 0, H)
+        gather(5, picked1[:, 6, :], 0, H)
+        interleave(on_scalar, 1, picked1[:, 5:7, :], 0, H, 0, 2)
+        gather(6, picked1[:, 2, :], 0, H)
         whole = range(SPLIT, NT)
         for q in range(2):
             multiply_quarter(0, q)
@@ -174,15 +172,16 @@ def tile_list_heads_gelu_kernel(tc, xT, w_words, w_scales, wgt, b, offs, out):
         for t in whole:
             multiply_whole(0, t)
         for q in range(2):
-            gather(7, picked67[:, 1, q * Q : (q + 1) * Q], q * Q, Q)
-            interleave(on_scalar, 1, picked67[:, 0:2, q * Q : (q + 1) * Q], q * Q, Q, 2, 4)
-        gather(7, picked67[:, 2, :], H, H)
+            gather(7, picked1[:, 3, q * Q : (q + 1) * Q], q * Q, Q)
+            interleave(on_scalar, 1, picked1[:, 2:4, q * Q : (q + 1) * Q], q * Q, Q, 2, 4)
+        gather(7, picked1[:, 4, :], H, H)
         for q in range(2):
             quantize(1, q * Q, Q)
+        gather(5, picked1[:, 2, :], H, H)
         for q in range(2):
-            gather(6, picked67[:, 1, q * Q : (q + 1) * Q], H + q * Q, Q)
+            gather(6, picked1[:, 3, q * Q : (q + 1) * Q], H + q * Q, Q)
         for q in range(2):
-            interleave(on_vector, 1, picked67[:, 1:3, q * Q : (q + 1) * Q], H + q * Q, Q, 2, 4)
+            interleave(on_vector, 1, picked1[:, 1:5, q * Q : (q + 1) * Q], H + q * Q, Q, 0, 4)
         for q in range(2):
             quantize(1, H + q * Q, Q)
 
@@ -198,15 +197,15 @@ def tile_list_heads_gelu_kernel(tc, xT, w_words, w_scales, wgt, b, offs, out):
         for s in range(2):
             finish(halves[0][u][:, s, :], 2 * u + s, 0, H)
         store(2 * u, 2, 0, H)
-        for t in whole:
-            multiply_whole(1, t)
-            finish(acc[t][:], t, 0, S)
-            store(t, 1, 0, S)
         for u in range(pairs - 1):
             multiply_half(1, 1, u)
             for s in range(2):
                 finish(halves[1][u][:, s, :], 2 * u + s, H, H)
             store(2 * u, 2, H, H)
+            t = SPLIT + u
+            multiply_whole(1, t)
+            finish(acc[t][:], t, 0, S)
+            store(t, 1, 0, S)
         u = pairs - 1
         multiply_half(1, 1, u, opens=1)
         multiply_half(0, 1, u, opens=1)

@@ -20,11 +20,15 @@ GELU = mybir.ActivationFunctionType.Gelu_apprx_tanh
 P = 128
 PASSES = 2
 PACK = 4
-NT = N_OUT // P
-H = S // 2
-Q = S // 4
-FOUR = 4
+TILES = N_OUT // P
+HALF = S // 2
+QUARTER = S // 4
+EARLY = 4
 SPLIT = 6
+PAIRS = SPLIT // 2
+LAST_PAIR = PAIRS - 1
+LIST_ROWS = 16
+RUN = 4
 
 
 def tile_list_heads_gelu_kernel(tc, xT, w_words, w_scales, wgt, b, offs, out):
@@ -33,77 +37,81 @@ def tile_list_heads_gelu_kernel(tc, xT, w_words, w_scales, wgt, b, offs, out):
         keep = ctx.enter_context(tc.tile_pool(name="keep", bufs=1))
         psum = ctx.enter_context(tc.psum_pool(name="psum", bufs=1))
 
-        lists = keep.tile([P, S // 16], U16, name="lists")
+        lists = keep.tile([P, S // LIST_ROWS], U16, name="lists")
         wg = keep.tile([P, S], F32, name="wg")
-        planes = [keep.tile([P, T], F32, name=f"plane{i}") for i in range(PASSES * PACK)]
+        planes = [keep.tile([P, T], F32, name=f"plane{n}") for n in range(PASSES * PACK)]
         w_sb = keep.tile([P, PASSES, 2 * N_OUT], U8, name="w_sb", align_bytes=256)
         ws_sb = keep.tile([P, PASSES, N_OUT], U8, name="ws_sb", align_bytes=256)
         b_rows = keep.tile([P, P], F32, name="b_rows")
-        b_cols = keep.tile([P, NT], F32, name="b_cols")
+        b_cols = keep.tile([P, TILES], F32, name="b_cols")
         ident = keep.tile([P, P], F32, name="ident")
-        warm = keep.tile([P, 1], F32, name="warm")
+        zero = keep.tile([P, 1], F32, name="zero")
         picked0 = keep.tile([P, PACK, S], F32, name="picked0")
-        picked1 = keep.tile([P, 7, H], F32, name="picked1")
+        picked1 = keep.tile([P, 6, HALF], F32, name="picked1")
         grouped = [keep.tile([P, S, PACK], BF16, name=f"grouped{a}", align_bytes=256) for a in range(PASSES)]
         codes = [keep.tile([P, S], U32, name=f"codes{a}", align_bytes=256) for a in range(PASSES)]
         scales = [keep.tile([P, S], U8, name=f"scales{a}", align_bytes=256) for a in range(PASSES)]
-        result = keep.tile([P, NT, S], F32, name="result")
-        quarters = [psum.tile([P, FOUR, Q], F32, name=f"quarter{q}") for q in range(2)]
-        halves = [{2: psum.tile([P, 2, H], F32, name="half02")}, {u: psum.tile([P, 2, H], F32, name=f"half1{u}") for u in range(3)}]
-        acc = {t: psum.tile([P, S], F32, name=f"acc{t}") for t in range(SPLIT, NT)}
+        result = keep.tile([P, TILES, S], F32, name="result")
+
+        quarter_bank = [psum.tile([P, EARLY, QUARTER], F32, name=f"quarter{q}") for q in range(2)]
+        first_half_bank = psum.tile([P, 2, HALF], F32, name="first_half")
+        second_half_bank = [psum.tile([P, 2, HALF], F32, name=f"second_half{u}") for u in range(LAST_PAIR)]
+        second_half_bank.append(quarter_bank[0][:].rearrange("p (s r) c -> p s (r c)", s=2))
+        whole_bank = {t: psum.tile([P, S], F32, name=f"whole{t}") for t in range(SPLIT, TILES)}
 
         x_view = xT.rearrange("(a p i) t -> a i p t", a=PASSES, i=PACK)
+        w_view = w_words.rearrange("a p n -> p a n")
+        out_view = out.rearrange("(t p) j -> p t j", p=P)
 
         def load_plane(n):
             nc.sync.dma_start(planes[n][:], x_view[n // PACK, n % PACK])
 
         def load_w_scales(a):
-            for q in range(4):
+            for g in range(4):
                 nc.sync.dma_start(
-                    ws_sb[32 * q : 32 * q + 4, a, :].bitcast(I32), w_scales[a, 4 * q : 4 * q + 4, :].bitcast(I32)
+                    ws_sb[32 * g : 32 * g + 4, a, :].bitcast(I32), w_scales[a, 4 * g : 4 * g + 4, :].bitcast(I32)
                 )
 
-        w_view = w_words.rearrange("a p n -> p a n")
-
-        def load_w(a0, a1, t0, t1):
+        def load_w(a, t0, t1):
             cols = slice(2 * P * t0, 2 * P * t1)
-            nc.sync.dma_start(w_sb[:, a0:a1, cols].bitcast(I32), w_view[:, a0:a1, cols].bitcast(I32))
+            nc.sync.dma_start(w_sb[:, a : a + 1, cols].bitcast(I32), w_view[:, a : a + 1, cols].bitcast(I32))
 
-        nc.vector.memset(b_rows[:], 0.0)
-        nc.vector.memset(warm[:], 0.0)
+        nc.vector.memset(b_rows[0 : P // 2, :], 0.0)
+        nc.vector.memset(zero[:], 0.0)
         nc.vector.memset(ws_sb[:].rearrange("p a n -> p (a n)").bitcast(I32), 0)
-        nc.scalar.dma_start(b_rows[0:NT, :], b.rearrange("(c p) -> c p", p=P))
-        nc.scalar.activation(warm[:], warm[:], GELU)
+        nc.scalar.dma_start(b_rows[0:TILES, :], b.rearrange("(c p) -> c p", p=P))
+        nc.scalar.activation(b_rows[P // 2 : P, :], zero[P // 2 : P, :].to_broadcast([P // 2, P]), GELU)
+
         load_plane(0)
         nc.sync.dma_start(lists[:], offs)
-        nc.sync.dma_start(wg[:, 0:Q], wgt[:, 0:Q])
-        nc.sync.dma_start(wg[:, Q:S], wgt[:, Q:S])
-        for n in range(1, 5):
+        nc.sync.dma_start(wg[:, 0:QUARTER], wgt[:, 0:QUARTER])
+        nc.sync.dma_start(wg[:, QUARTER:S], wgt[:, QUARTER:S])
+        for n in range(1, PACK + 1):
             load_plane(n)
         load_w_scales(0)
-        load_w(0, 1, 0, 4)
-        for n in range(5, 8):
+        load_w(0, 0, EARLY)
+        for n in range(PACK + 1, PASSES * PACK):
             load_plane(n)
-        load_w(0, 1, FOUR, NT)
+        load_w(0, EARLY, TILES)
         load_w_scales(1)
-        load_w(1, 2, 0, FOUR)
-        load_w(1, 2, FOUR, NT)
+        load_w(1, 0, EARLY)
+        load_w(1, EARLY, TILES)
 
         make_identity(nc, ident[:])
-        nc.tensor.transpose(acc[NT - 1][:, 0:P], b_rows[:], ident[:])
-        nc.scalar.copy(b_cols[:], acc[NT - 1][:, 0:NT])
+        nc.tensor.transpose(whole_bank[TILES - 1][:, 0:P], b_rows[:], ident[:])
+        nc.scalar.copy(b_cols[:], whole_bank[TILES - 1][:, 0:TILES])
 
         def gather(n, dst, c0, cn):
             nc.vector.tensor_tensor(
                 dst,
-                planes[n][:].indirect(lists[:, c0 // 16 : (c0 + cn) // 16]),
+                planes[n][:].indirect(lists[:, c0 // LIST_ROWS : (c0 + cn) // LIST_ROWS]),
                 wg[:, c0 : c0 + cn],
                 MULT,
             )
 
         def interleave(copy, a, src, c0, cn, i0, i1):
-            dst = grouped[a][:, c0 : c0 + cn, i0:i1].rearrange("p (c j) i -> p c i j", j=4)
-            copy(dst, src.rearrange("p i (c j) -> p c i j", j=4))
+            dst = grouped[a][:, c0 : c0 + cn, i0:i1].rearrange("p (c j) i -> p c i j", j=RUN)
+            copy(dst, src.rearrange("p i (c j) -> p c i j", j=RUN))
 
         def quantize(a, c0, cn):
             nc.vector.quantize_mx(
@@ -112,32 +120,29 @@ def tile_list_heads_gelu_kernel(tc, xT, w_words, w_scales, wgt, b, offs, out):
                 in_=grouped[a][:, c0 : c0 + cn, :].rearrange("p c i -> p (c i)"),
             )
 
-        def multiply(dst, a, t, c0, cn, start, stop):
+        def multiply(dst, a, t, c0, cn, first, last):
             nc.tensor.matmul_mx(
                 out=dst,
                 lhsT=w_sb[:, a, 2 * P * t : 2 * P * (t + 1)].bitcast(FP4X4),
                 lhsT_scale=ws_sb[:, a, P * t : P * (t + 1)],
                 rhs=codes[a][:, c0 : c0 + cn].bitcast(FP8X4),
                 rhs_scale=scales[a][:, c0 : c0 + cn],
-                start=start,
-                stop=stop,
+                start=first and a == 0,
+                stop=last and a == PASSES - 1,
             )
 
         def multiply_whole(a, t):
-            multiply(acc[t][:], a, t, 0, S, a == 0, a == PASSES - 1)
-
-        def multiply_half(a, h, u, opens=0):
-            for q in range(2):
-                for s in range(2):
-                    first = a == opens and q == 0 and s == 0
-                    last = a != opens and q == 1 and s == 1
-                    multiply(halves[h][u][:, s, q * Q : (q + 1) * Q], a, 2 * u + s, h * H + q * Q, Q, first, last)
+            multiply(whole_bank[t][:], a, t, 0, S, True, True)
 
         def multiply_quarter(a, q):
-            for t in range(FOUR):
-                multiply(quarters[q][:, t, :], a, t, q * Q, Q, a == 0 and t == 0, a == 1 and t == FOUR - 1)
+            for t in range(EARLY):
+                multiply(quarter_bank[q][:, t, :], a, t, q * QUARTER, QUARTER, t == 0, t == EARLY - 1)
 
-        out_view = out.rearrange("(t p) j -> p t j", p=P)
+        def multiply_half(bank, a, u, c0):
+            for q in range(2):
+                for s in range(2):
+                    dst = bank[:, s, q * QUARTER : (q + 1) * QUARTER]
+                    multiply(dst, a, 2 * u + s, c0 + q * QUARTER, QUARTER, q + s == 0, q + s == 2)
 
         def finish(src, t, c0, cn):
             nc.scalar.activation(result[:, t, c0 : c0 + cn], src, GELU, bias=b_cols[:, t : t + 1])
@@ -146,70 +151,68 @@ def tile_list_heads_gelu_kernel(tc, xT, w_words, w_scales, wgt, b, offs, out):
             nc.sync.dma_start(out_view[:, t0 : t0 + tn, c0 : c0 + cn], result[:, t0 : t0 + tn, c0 : c0 + cn])
 
         on_scalar, on_vector = nc.scalar.copy, nc.vector.tensor_copy
-        pairs = SPLIT // 2
 
-        gather(0, picked0[:, 0, 0:Q], 0, Q)
-        gather(0, picked0[:, 0, Q:S], Q, S - Q)
+        gather(0, picked0[:, 0, 0:QUARTER], 0, QUARTER)
+        gather(0, picked0[:, 0, QUARTER:S], QUARTER, S - QUARTER)
         gather(1, picked0[:, 1, :], 0, S)
         interleave(on_scalar, 0, picked0[:, 0:2, :], 0, S, 0, 2)
         gather(2, picked0[:, 2, :], 0, S)
-        for h in range(2):
-            gather(3, picked0[:, 3, h * H : (h + 1) * H], h * H, H)
-            interleave(on_scalar, 0, picked0[:, 2:4, h * H : (h + 1) * H], h * H, H, 2, 4)
-        gather(4, picked1[:, 5, :], 0, H)
-        quantize(0, 0, H)
-        gather(4, picked1[:, 1, :], H, H)
-        quantize(0, H, H)
-        gather(5, picked1[:, 6, :], 0, H)
-        interleave(on_scalar, 1, picked1[:, 5:7, :], 0, H, 0, 2)
-        gather(6, picked1[:, 2, :], 0, H)
-        whole = range(SPLIT, NT)
+        for c0 in (0, HALF):
+            gather(3, picked0[:, 3, c0 : c0 + HALF], c0, HALF)
+            interleave(on_scalar, 0, picked0[:, 2:4, c0 : c0 + HALF], c0, HALF, 2, 4)
+
+        gather(4, picked1[:, 4, :], 0, HALF)
+        quantize(0, 0, HALF)
+        gather(4, picked1[:, 0, :], HALF, HALF)
+        quantize(0, HALF, HALF)
+        gather(5, picked1[:, 5, :], 0, HALF)
+        interleave(on_scalar, 1, picked1[:, 4:6, :], 0, HALF, 0, 2)
+        gather(6, picked1[:, 1, :], 0, HALF)
         for q in range(2):
             multiply_quarter(0, q)
-        for u in range(pairs - 1):
-            multiply_half(0, 1, u)
-        multiply_half(0, 0, pairs - 1)
-        for t in whole:
+        for u in range(LAST_PAIR):
+            multiply_half(second_half_bank[u], 0, u, HALF)
+        multiply_half(first_half_bank, 0, LAST_PAIR, 0)
+        for t in whole_bank:
             multiply_whole(0, t)
-        for q in range(2):
-            gather(7, picked1[:, 3, q * Q : (q + 1) * Q], q * Q, Q)
-            interleave(on_scalar, 1, picked1[:, 2:4, q * Q : (q + 1) * Q], q * Q, Q, 2, 4)
-        gather(7, picked1[:, 4, :], H, H)
-        for q in range(2):
-            quantize(1, q * Q, Q)
-        gather(5, picked1[:, 2, :], H, H)
-        for q in range(2):
-            gather(6, picked1[:, 3, q * Q : (q + 1) * Q], H + q * Q, Q)
-        for q in range(2):
-            interleave(on_vector, 1, picked1[:, 1:5, q * Q : (q + 1) * Q], H + q * Q, Q, 0, 4)
-        for q in range(2):
-            quantize(1, H + q * Q, Q)
+        for c0 in (0, QUARTER):
+            gather(7, picked1[:, 2, c0 : c0 + QUARTER], c0, QUARTER)
+            interleave(on_scalar, 1, picked1[:, 1:3, c0 : c0 + QUARTER], c0, QUARTER, 2, 4)
+        gather(7, picked1[:, 3, :], HALF, HALF)
+        for c0 in (0, QUARTER):
+            quantize(1, c0, QUARTER)
+        gather(5, picked1[:, 1, :], HALF, HALF)
+        for c0 in (0, QUARTER):
+            gather(6, picked1[:, 2, c0 : c0 + QUARTER], HALF + c0, QUARTER)
+        for c0 in (0, QUARTER):
+            interleave(on_vector, 1, picked1[:, 0:4, c0 : c0 + QUARTER], HALF + c0, QUARTER, 0, 4)
+        for c0 in (0, QUARTER):
+            quantize(1, HALF + c0, QUARTER)
 
         for q in range(2):
             multiply_quarter(1, q)
-            for t in range(FOUR):
-                finish(quarters[q][:, t, :], t, q * Q, Q)
+            for t in range(EARLY):
+                finish(quarter_bank[q][:, t, :], t, q * QUARTER, QUARTER)
                 if q == 1 and t < 2:
-                    store(t, 1, 0, H)
-        store(2, 2, 0, H)
-        u = pairs - 1
-        multiply_half(1, 0, u)
+                    store(t, 1, 0, HALF)
+        store(2, 2, 0, HALF)
+        multiply_half(first_half_bank, 1, LAST_PAIR, 0)
         for s in range(2):
-            finish(halves[0][u][:, s, :], 2 * u + s, 0, H)
-        store(2 * u, 2, 0, H)
-        for u in range(pairs - 1):
-            multiply_half(1, 1, u)
+            finish(first_half_bank[:, s, :], 2 * LAST_PAIR + s, 0, HALF)
+        store(2 * LAST_PAIR, 2, 0, HALF)
+        multiply_half(second_half_bank[LAST_PAIR], 0, LAST_PAIR, HALF)
+
+        for u in range(LAST_PAIR):
+            multiply_half(second_half_bank[u], 1, u, HALF)
             for s in range(2):
-                finish(halves[1][u][:, s, :], 2 * u + s, H, H)
-            store(2 * u, 2, H, H)
+                finish(second_half_bank[u][:, s, :], 2 * u + s, HALF, HALF)
+            store(2 * u, 2, HALF, HALF)
             t = SPLIT + u
             multiply_whole(1, t)
-            finish(acc[t][:], t, 0, S)
+            finish(whole_bank[t][:], t, 0, S)
             store(t, 1, 0, S)
-        u = pairs - 1
-        multiply_half(1, 1, u, opens=1)
-        multiply_half(0, 1, u, opens=1)
-        finish(halves[1][u][:, 0, :], 2 * u, H, H)
-        store(2 * u, 1, H, H)
-        finish(halves[1][u][:, 1, :], 2 * u + 1, H, H)
-        nc.scalar.dma_start(out_view[:, 2 * u + 1, H:S], result[:, 2 * u + 1, H:S])
+        multiply_half(second_half_bank[LAST_PAIR], 1, LAST_PAIR, HALF)
+        finish(second_half_bank[LAST_PAIR][:, 0, :], SPLIT - 2, HALF, HALF)
+        store(SPLIT - 2, 1, HALF, HALF)
+        finish(second_half_bank[LAST_PAIR][:, 1, :], SPLIT - 1, HALF, HALF)
+        nc.scalar.dma_start(out_view[:, SPLIT - 1, HALF:S], result[:, SPLIT - 1, HALF:S])

@@ -53,10 +53,10 @@ def tile_list_heads_gelu_kernel(tc, xT, w_words, w_scales, wgt, b, offs, out):
         scales = [keep.tile([P, S], U8, name=f"scales{a}", align_bytes=256) for a in range(PASSES)]
         result = keep.tile([P, TILES, S], F32, name="result")
 
-        quarter_bank = [psum.tile([P, EARLY, QUARTER], F32, name=f"quarter{q}") for q in range(2)]
-        first_half_bank = psum.tile([P, 2, HALF], F32, name="first_half")
+        quarter_bank = [psum.tile([P, 2, HALF], F32, name=f"quarter{q}") for q in range(2)]
+        first_half_bank = {u: psum.tile([P, 2, HALF], F32, name=f"first_half{u}") for u in range(1, PAIRS)}
         second_half_bank = [psum.tile([P, 2, HALF], F32, name=f"second_half{u}") for u in range(LAST_PAIR)]
-        second_half_bank.append(quarter_bank[0][:].rearrange("p (s r) c -> p s (r c)", s=2))
+        second_half_bank.append(quarter_bank[0])
         whole_bank = {t: psum.tile([P, S], F32, name=f"whole{t}") for t in range(SPLIT, TILES)}
 
         x_view = xT.rearrange("(a p i) t -> a i p t", a=PASSES, i=PACK)
@@ -135,8 +135,8 @@ def tile_list_heads_gelu_kernel(tc, xT, w_words, w_scales, wgt, b, offs, out):
             multiply(whole_bank[t][:], a, t, 0, S, True, True)
 
         def multiply_quarter(a, q):
-            for t in range(EARLY):
-                multiply(quarter_bank[q][:, t, :], a, t, q * QUARTER, QUARTER, t == 0, t == EARLY - 1)
+            for t in range(2):
+                multiply(quarter_bank[q][:, t, 0:QUARTER], a, t, q * QUARTER, QUARTER, t == 0, t == 1)
 
         def multiply_half(bank, a, u, c0):
             for q in range(2):
@@ -170,9 +170,10 @@ def tile_list_heads_gelu_kernel(tc, xT, w_words, w_scales, wgt, b, offs, out):
         gather(6, picked1[:, 1, :], 0, HALF)
         for q in range(2):
             multiply_quarter(0, q)
+        multiply_half(first_half_bank[1], 0, 1, 0)
         for u in range(LAST_PAIR):
             multiply_half(second_half_bank[u], 0, u, HALF)
-        multiply_half(first_half_bank, 0, LAST_PAIR, 0)
+        multiply_half(first_half_bank[LAST_PAIR], 0, LAST_PAIR, 0)
         for t in whole_bank:
             multiply_whole(0, t)
         for c0 in (0, QUARTER):
@@ -191,23 +192,23 @@ def tile_list_heads_gelu_kernel(tc, xT, w_words, w_scales, wgt, b, offs, out):
 
         for q in range(2):
             multiply_quarter(1, q)
-            for t in range(EARLY):
-                finish(quarter_bank[q][:, t, :], t, q * QUARTER, QUARTER)
-                if q == 1 and t < 2:
+            for t in range(2):
+                finish(quarter_bank[q][:, t, 0:QUARTER], t, q * QUARTER, QUARTER)
+                if q == 1:
                     store(t, 1, 0, HALF)
-        store(2, 2, 0, HALF)
-        multiply_half(first_half_bank, 1, LAST_PAIR, 0)
-        for s in range(2):
-            finish(first_half_bank[:, s, :], 2 * LAST_PAIR + s, 0, HALF)
-        store(2 * LAST_PAIR, 2, 0, HALF)
+        for u in range(1, PAIRS):
+            multiply_half(first_half_bank[u], 1, u, 0)
+            for s in range(2):
+                finish(first_half_bank[u][:, s, :], 2 * u + s, 0, HALF)
+            store(2 * u, 2, 0, HALF)
         multiply_half(second_half_bank[LAST_PAIR], 0, LAST_PAIR, HALF)
 
         for u in range(LAST_PAIR):
             multiply_half(second_half_bank[u], 1, u, HALF)
             for s in range(2):
                 finish(second_half_bank[u][:, s, :], 2 * u + s, HALF, HALF)
-            store(2 * u, 2, HALF, HALF)
-            t = SPLIT + u
+                store(2 * u + s, 1, HALF, HALF)
+        for t in whole_bank:
             multiply_whole(1, t)
             finish(whole_bank[t][:], t, 0, S)
             store(t, 1, 0, S)

@@ -194,13 +194,12 @@ def tile_list_heads_gelu_kernel(tc, xT, w_words, w_scales, wgt, b, offs, out):
             multiply_quarter(1, q)
             for t in range(2):
                 finish(quarter_bank[q][:, t, 0:QUARTER], t, q * QUARTER, QUARTER)
-                if q == 1:
-                    store(t, 1, 0, HALF)
+            store(0, 2, q * QUARTER, QUARTER)
         for u in range(1, PAIRS):
             multiply_half(first_half_bank[u], 1, u, 0)
             for s in range(2):
                 finish(first_half_bank[u][:, s, :], 2 * u + s, 0, HALF)
-            store(2 * u, 2, 0, HALF)
+                store(2 * u + s, 1, 0, HALF)
         multiply_half(second_half_bank[LAST_PAIR], 0, LAST_PAIR, HALF)
 
         for u in range(LAST_PAIR):

@@ -79,14 +79,15 @@ def tile_list_heads_gelu_kernel(tc, xT, w_words, w_scales, wgt, b, offs, out):
         nc.vector.memset(b_rows[0 : P // 2, :], 0.0)
         nc.vector.memset(zero[:], 0.0)
         nc.vector.memset(ws_sb[:].rearrange("p a n -> p (a n)").bitcast(I32), 0)
-        nc.scalar.dma_start(b_rows[0:TILES, :], b.rearrange("(c p) -> c p", p=P))
         nc.scalar.activation(b_rows[P // 2 : P, :], zero[P // 2 : P, :].to_broadcast([P // 2, P]), GELU)
 
         load_plane(0)
         nc.sync.dma_start(lists[:], offs)
         nc.sync.dma_start(wg[:, 0:QUARTER], wgt[:, 0:QUARTER])
         nc.sync.dma_start(wg[:, QUARTER:S], wgt[:, QUARTER:S])
-        for n in range(1, PACK + 1):
+        load_plane(1)
+        nc.sync.dma_start(b_rows[0:TILES, :], b.rearrange("(c p) -> c p", p=P))
+        for n in range(2, PACK + 1):
             load_plane(n)
         load_w_scales(0)
         load_w(0, 0, EARLY)
@@ -139,6 +140,10 @@ def tile_list_heads_gelu_kernel(tc, xT, w_words, w_scales, wgt, b, offs, out):
                 multiply(quarter_bank[q][:, t, 0:QUARTER], a, t, q * QUARTER, QUARTER, t == 0, t == 1)
 
         def multiply_half(bank, a, u, c0):
+            if a == 0:
+                for s in range(2):
+                    multiply(bank[:, s, :], a, 2 * u + s, c0, HALF, s == 0, s == 1)
+                return
             for q in range(2):
                 for s in range(2):
                     dst = bank[:, s, q * QUARTER : (q + 1) * QUARTER]

@@ -139,6 +139,10 @@ def tile_list_heads_gelu_kernel(tc, xT, w_words, w_scales, wgt, b, offs, out):
             for t in range(2):
                 multiply(quarter_bank[q][:, t, 0:QUARTER], a, t, q * QUARTER, QUARTER, t == 0, t == 1)
 
+        def multiply_late(bank, a, q):
+            for t in range(2):
+                multiply(bank[:, t, 0:QUARTER], a, t, q * QUARTER, QUARTER, t == 0, t == 1)
+
         def multiply_half(bank, a, u, c0):
             if a == 0:
                 for s in range(2):
@@ -176,8 +180,8 @@ def tile_list_heads_gelu_kernel(tc, xT, w_words, w_scales, wgt, b, offs, out):
         for q in range(2):
             multiply_quarter(0, q)
         multiply_half(first_half_bank[1], 0, 1, 0)
-        for u in range(LAST_PAIR):
-            multiply_half(second_half_bank[u], 0, u, HALF)
+        multiply_late(second_half_bank[0], 0, 2)
+        multiply_half(second_half_bank[1], 0, 1, HALF)
         multiply_half(first_half_bank[LAST_PAIR], 0, LAST_PAIR, 0)
         for t in whole_bank:
             multiply_whole(0, t)
@@ -205,9 +209,15 @@ def tile_list_heads_gelu_kernel(tc, xT, w_words, w_scales, wgt, b, offs, out):
             for s in range(2):
                 finish(first_half_bank[u][:, s, :], 2 * u + s, 0, HALF)
                 store(2 * u + s, 1, 0, HALF)
+        multiply_late(quarter_bank[1], 0, 3)
         multiply_half(second_half_bank[LAST_PAIR], 0, LAST_PAIR, HALF)
 
-        for u in range(LAST_PAIR):
+        for q, bank in ((2, second_half_bank[0]), (3, quarter_bank[1])):
+            multiply_late(bank, 1, q)
+            for t in range(2):
+                finish(bank[:, t, 0:QUARTER], t, q * QUARTER, QUARTER)
+            store(0, 2, q * QUARTER, QUARTER)
+        for u in range(1, LAST_PAIR):
             multiply_half(second_half_bank[u], 1, u, HALF)
             for s in range(2):
                 finish(second_half_bank[u][:, s, :], 2 * u + s, HALF, HALF)

@@ -47,7 +47,7 @@ def tile_list_heads_gelu_kernel(tc, xT, w_words, w_scales, wgt, b, offs, out):
         ident = keep.tile([P, P], F32, name="ident")
         zero = keep.tile([P, 1], F32, name="zero")
         picked0 = keep.tile([P, PACK, S], F32, name="picked0")
-        picked1 = keep.tile([P, 6, HALF], F32, name="picked1")
+        picked1 = keep.tile([P, PACK * S], F32, name="picked1")
         grouped = [keep.tile([P, S, PACK], BF16, name=f"grouped{a}", align_bytes=256) for a in range(PASSES)]
         codes = [keep.tile([P, S], U32, name=f"codes{a}", align_bytes=256) for a in range(PASSES)]
         scales = [keep.tile([P, S], U8, name=f"scales{a}", align_bytes=256) for a in range(PASSES)]
@@ -170,13 +170,22 @@ def tile_list_heads_gelu_kernel(tc, xT, w_words, w_scales, wgt, b, offs, out):
             gather(3, picked0[:, 3, c0 : c0 + HALF], c0, HALF)
             interleave(on_scalar, 0, picked0[:, 2:4, c0 : c0 + HALF], c0, HALF, 2, 4)
 
-        gather(4, picked1[:, 4, :], 0, HALF)
+        rows = picked1[:].rearrange("p (i j) -> p i j", i=PACK)
+        borrowed6 = S + 3 * QUARTER
+        to_borrowed7 = 3 * QUARTER
+
+        def early_pair(q):
+            c0 = borrowed6 + q * QUARTER
+            return picked1[:, c0 : c0 + 2 * to_borrowed7].rearrange("p (i j) -> p i j", i=2)[:, :, 0:QUARTER]
+
+        gather(4, rows[:, 0, 0 : 3 * QUARTER], 0, 3 * QUARTER)
         quantize(0, 0, HALF)
-        gather(4, picked1[:, 0, :], HALF, HALF)
+        gather(4, rows[:, 0, 3 * QUARTER : S], 3 * QUARTER, QUARTER)
+        gather(5, rows[:, 1, 0:HALF], 0, HALF)
+        interleave(on_scalar, 1, rows[:, 0:2, 0:HALF], 0, HALF, 0, 2)
         quantize(0, HALF, HALF)
-        gather(5, picked1[:, 5, :], 0, HALF)
-        interleave(on_scalar, 1, picked1[:, 4:6, :], 0, HALF, 0, 2)
-        gather(6, picked1[:, 1, :], 0, HALF)
+        gather(5, rows[:, 1, HALF : 3 * QUARTER], HALF, QUARTER)
+        gather(6, picked1[:, borrowed6 : borrowed6 + HALF], 0, HALF)
         for q in range(2):
             multiply_quarter(0, q)
         multiply_half(first_half_bank[1], 0, 1, 0)
@@ -185,19 +194,19 @@ def tile_list_heads_gelu_kernel(tc, xT, w_words, w_scales, wgt, b, offs, out):
         multiply_half(first_half_bank[LAST_PAIR], 0, LAST_PAIR, 0)
         for t in whole_bank:
             multiply_whole(0, t)
-        for c0 in (0, QUARTER):
-            gather(7, picked1[:, 2, c0 : c0 + QUARTER], c0, QUARTER)
-            interleave(on_scalar, 1, picked1[:, 1:3, c0 : c0 + QUARTER], c0, QUARTER, 2, 4)
-        gather(7, picked1[:, 3, :], HALF, HALF)
+        for q in range(2):
+            gather(7, early_pair(q)[:, 1, :], q * QUARTER, QUARTER)
+            interleave(on_scalar, 1, early_pair(q), q * QUARTER, QUARTER, 2, 4)
+        gather(7, rows[:, 3, HALF:S], HALF, HALF)
         for c0 in (0, QUARTER):
             quantize(1, c0, QUARTER)
-        gather(5, picked1[:, 1, :], HALF, HALF)
-        for c0 in (0, QUARTER):
-            gather(6, picked1[:, 2, c0 : c0 + QUARTER], HALF + c0, QUARTER)
-        for c0 in (0, QUARTER):
-            interleave(on_vector, 1, picked1[:, 0:4, c0 : c0 + QUARTER], HALF + c0, QUARTER, 0, 4)
-        for c0 in (0, QUARTER):
-            quantize(1, HALF + c0, QUARTER)
+        gather(5, rows[:, 1, 3 * QUARTER : S], 3 * QUARTER, QUARTER)
+        for c0 in (HALF, 3 * QUARTER):
+            gather(6, rows[:, 2, c0 : c0 + QUARTER], c0, QUARTER)
+        for c0 in (HALF, 3 * QUARTER):
+            interleave(on_vector, 1, rows[:, :, c0 : c0 + QUARTER], c0, QUARTER, 0, 4)
+        for c0 in (HALF, 3 * QUARTER):
+            quantize(1, c0, QUARTER)
 
         for q in range(2):
             multiply_quarter(1, q)

@@ -28,6 +28,8 @@ SPLIT = 6
 PAIRS = SPLIT // 2
 LAST_PAIR = PAIRS - 1
 LIST_ROWS = 16
+BLOCK = 32
+REPEAT = 8
 RUN = 4
 
 
@@ -38,7 +40,10 @@ def tile_list_heads_gelu_kernel(tc, xT, w_words, w_scales, wgt, b, offs, out):
         psum = ctx.enter_context(tc.psum_pool(name="psum", bufs=1))
 
         lists = keep.tile([P, S // LIST_ROWS], U16, name="lists")
-        wg = keep.tile([P, S], F32, name="wg")
+        wg = keep.tile([P, S], F32, name="wg", align_bytes=64)
+        wg_runs = keep.tile([P, BLOCK], F32, name="wg_runs", align_bytes=64)
+        wg_picks = keep.tile([P, BLOCK], F32, name="wg_picks", align_bytes=64)
+        wg_turned = keep.tile([P, HALF], F32, name="wg_turned", align_bytes=64)
         planes = [keep.tile([P, T], F32, name=f"plane{n}") for n in range(PASSES * PACK)]
         w_sb = keep.tile([P, PASSES, 2 * N_OUT], U8, name="w_sb", align_bytes=256)
         ws_sb = keep.tile([P, PASSES, N_OUT], U8, name="ws_sb", align_bytes=256)
@@ -81,10 +86,11 @@ def tile_list_heads_gelu_kernel(tc, xT, w_words, w_scales, wgt, b, offs, out):
         nc.vector.memset(ws_sb[:].rearrange("p a n -> p (a n)").bitcast(I32), 0)
         nc.scalar.activation(b_rows[P // 2 : P, :], zero[P // 2 : P, :].to_broadcast([P // 2, P]), GELU)
 
+        runs = HALF // BLOCK
+        nc.sync.dma_start(wg_runs[:], wgt.rearrange("(m r) (J b) -> r m J b", r=REPEAT, b=BLOCK)[0][:, 0:runs, :])
         load_plane(0)
         nc.sync.dma_start(lists[:], offs)
-        nc.sync.dma_start(wg[:, 0:QUARTER], wgt[:, 0:QUARTER])
-        nc.sync.dma_start(wg[:, QUARTER:S], wgt[:, QUARTER:S])
+        nc.sync.dma_start(wg[:, HALF:S], wgt[:, HALF:S])
         load_plane(1)
         nc.sync.dma_start(b_rows[0:TILES, :], b.rearrange("(c p) -> c p", p=P))
         for n in range(2, PACK + 1):
@@ -101,6 +107,20 @@ def tile_list_heads_gelu_kernel(tc, xT, w_words, w_scales, wgt, b, offs, out):
         make_identity(nc, ident[:])
         nc.tensor.transpose(whole_bank[TILES - 1][:, 0:P], b_rows[:], ident[:])
         nc.scalar.copy(b_cols[:], whole_bank[TILES - 1][:, 0:TILES])
+
+        nc.vector.transpose(wg_picks[:], wg_runs[:])
+        by_run = wg_picks[:].rearrange("p (m J) -> p J m", J=runs)
+        rows_in_block = BLOCK // REPEAT
+        quarter_runs = QUARTER // BLOCK
+        for q in range(2):
+            nc.vector.tensor_copy(
+                wg_turned[:, q * QUARTER : (q + 1) * QUARTER].rearrange("p (J m r) -> p J m r", m=rows_in_block, r=REPEAT),
+                by_run[:, q * quarter_runs : (q + 1) * quarter_runs, :]
+                .unsqueeze(3)
+                .to_broadcast([P, quarter_runs, rows_in_block, REPEAT]),
+            )
+        for q in range(2):
+            nc.vector.transpose(wg[:, q * QUARTER : (q + 1) * QUARTER], wg_turned[:, q * QUARTER : (q + 1) * QUARTER])
 
         def gather(n, dst, c0, cn):
             nc.vector.tensor_tensor(
@@ -185,6 +205,7 @@ def tile_list_heads_gelu_kernel(tc, xT, w_words, w_scales, wgt, b, offs, out):
         interleave(on_scalar, 1, rows[:, 0:2, 0:HALF], 0, HALF, 0, 2)
         quantize(0, HALF, HALF)
         gather(5, rows[:, 1, HALF : 3 * QUARTER], HALF, QUARTER)
+        interleave(on_scalar, 1, rows[:, 0:2, HALF : 3 * QUARTER], HALF, QUARTER, 0, 2)
         gather(6, picked1[:, borrowed6 : borrowed6 + HALF], 0, HALF)
         for q in range(2):
             multiply_quarter(0, q)
@@ -203,8 +224,8 @@ def tile_list_heads_gelu_kernel(tc, xT, w_words, w_scales, wgt, b, offs, out):
         gather(5, rows[:, 1, 3 * QUARTER : S], 3 * QUARTER, QUARTER)
         for c0 in (HALF, 3 * QUARTER):
             gather(6, rows[:, 2, c0 : c0 + QUARTER], c0, QUARTER)
-        for c0 in (HALF, 3 * QUARTER):
-            interleave(on_vector, 1, rows[:, :, c0 : c0 + QUARTER], c0, QUARTER, 0, 4)
+        interleave(on_vector, 1, rows[:, 2:4, HALF : 3 * QUARTER], HALF, QUARTER, 2, 4)
+        interleave(on_vector, 1, rows[:, :, 3 * QUARTER : S], 3 * QUARTER, QUARTER, 0, 4)
         for c0 in (HALF, 3 * QUARTER):
             quantize(1, c0, QUARTER)
 

@@ -40,11 +40,11 @@ def tile_list_heads_gelu_kernel(tc, xT, w_words, w_scales, wgt, b, offs, out):
         psum = ctx.enter_context(tc.psum_pool(name="psum", bufs=1))
 
         lists = keep.tile([P, S // LIST_ROWS], U16, name="lists")
-        wg = keep.tile([P, S], F32, name="wg", align_bytes=64)
+        wg = keep.tile([P, S], F32, name="wg", align_bytes=256)
         wg_runs = keep.tile([P, BLOCK], F32, name="wg_runs", align_bytes=64)
         wg_picks = keep.tile([P, BLOCK], F32, name="wg_picks", align_bytes=64)
         wg_turned = keep.tile([P, HALF], F32, name="wg_turned", align_bytes=64)
-        planes = [keep.tile([P, T], F32, name=f"plane{n}") for n in range(PASSES * PACK)]
+        planes = [keep.tile([P, T], F32, name=f"plane{n}", align_bytes=256) for n in range(PASSES * PACK)]
         w_sb = keep.tile([P, PASSES, 2 * N_OUT], U8, name="w_sb", align_bytes=256)
         ws_sb = keep.tile([P, PASSES, N_OUT], U8, name="ws_sb", align_bytes=256)
         b_rows = keep.tile([P, P], F32, name="b_rows")
@@ -56,7 +56,7 @@ def tile_list_heads_gelu_kernel(tc, xT, w_words, w_scales, wgt, b, offs, out):
         grouped = [keep.tile([P, S, PACK], BF16, name=f"grouped{a}", align_bytes=256) for a in range(PASSES)]
         codes = [keep.tile([P, S], U32, name=f"codes{a}", align_bytes=256) for a in range(PASSES)]
         scales = [keep.tile([P, S], U8, name=f"scales{a}", align_bytes=256) for a in range(PASSES)]
-        result = keep.tile([P, TILES, S], F32, name="result")
+        result = keep.tile([P, TILES, S], F32, name="result", align_bytes=256)
 
         quarter_bank = [psum.tile([P, 2, HALF], F32, name=f"quarter{q}") for q in range(2)]
         first_half_bank = {u: psum.tile([P, 2, HALF], F32, name=f"first_half{u}") for u in range(1, PAIRS)}
@@ -205,7 +205,6 @@ def tile_list_heads_gelu_kernel(tc, xT, w_words, w_scales, wgt, b, offs, out):
         interleave(on_scalar, 1, rows[:, 0:2, 0:HALF], 0, HALF, 0, 2)
         quantize(0, HALF, HALF)
         gather(5, rows[:, 1, HALF : 3 * QUARTER], HALF, QUARTER)
-        interleave(on_scalar, 1, rows[:, 0:2, HALF : 3 * QUARTER], HALF, QUARTER, 0, 2)
         gather(6, picked1[:, borrowed6 : borrowed6 + HALF], 0, HALF)
         for q in range(2):
             multiply_quarter(0, q)
@@ -224,8 +223,8 @@ def tile_list_heads_gelu_kernel(tc, xT, w_words, w_scales, wgt, b, offs, out):
         gather(5, rows[:, 1, 3 * QUARTER : S], 3 * QUARTER, QUARTER)
         for c0 in (HALF, 3 * QUARTER):
             gather(6, rows[:, 2, c0 : c0 + QUARTER], c0, QUARTER)
-        interleave(on_vector, 1, rows[:, 2:4, HALF : 3 * QUARTER], HALF, QUARTER, 2, 4)
-        interleave(on_vector, 1, rows[:, :, 3 * QUARTER : S], 3 * QUARTER, QUARTER, 0, 4)
+        for c0 in (HALF, 3 * QUARTER):
+            interleave(on_vector, 1, rows[:, :, c0 : c0 + QUARTER], c0, QUARTER, 0, 4)
         for c0 in (HALF, 3 * QUARTER):
             quantize(1, c0, QUARTER)
 

from contextlib import ExitStack

import concourse.mybir as mybir
from concourse.masks import make_identity

K, N_OUT, T, S = 1024, 1024, 1024, 512
FLOPS = 2 * K * N_OUT * S

F32 = mybir.dt.float32
BF16 = mybir.dt.bfloat16
I32 = mybir.dt.int32
U32 = mybir.dt.uint32
U16 = mybir.dt.uint16
U8 = mybir.dt.uint8
FP8X4 = mybir.dt.float8_e4m3fn_x4
FP4X4 = mybir.dt.float4_e2m1fn_x4
MULT = mybir.AluOpType.mult
GELU = mybir.ActivationFunctionType.Gelu_apprx_tanh

P = 128
PASSES = 2
PACK = 4
TILES = N_OUT // P
HALF = S // 2
QUARTER = S // 4
EARLY = 4
SPLIT = 6
PAIRS = SPLIT // 2
LAST_PAIR = PAIRS - 1
LIST_ROWS = 16
BLOCK = 32
REPEAT = 8
RUN = 4


def tile_list_heads_gelu_kernel(tc, xT, w_words, w_scales, wgt, b, offs, out):
    nc = tc.nc
    with ExitStack() as ctx:
        keep = ctx.enter_context(tc.tile_pool(name="keep", bufs=1))
        psum = ctx.enter_context(tc.psum_pool(name="psum", bufs=1))

        lists = keep.tile([P, S // LIST_ROWS], U16, name="lists")
        wg = keep.tile([P, S], F32, name="wg", align_bytes=256)
        wg_runs = keep.tile([P, BLOCK], F32, name="wg_runs", align_bytes=64)
        wg_picks = keep.tile([P, BLOCK], F32, name="wg_picks", align_bytes=64)
        wg_turned = keep.tile([P, HALF], F32, name="wg_turned", align_bytes=64)
        planes = [keep.tile([P, T], F32, name=f"plane{n}", align_bytes=256) for n in range(PASSES * PACK)]
        w_sb = keep.tile([P, PASSES, 2 * N_OUT], U8, name="w_sb", align_bytes=256)
        ws_sb = keep.tile([P, PASSES, N_OUT], U8, name="ws_sb", align_bytes=256)
        b_rows = keep.tile([P, P], F32, name="b_rows")
        b_cols = keep.tile([P, TILES], F32, name="b_cols")
        ident = keep.tile([P, P], F32, name="ident")
        zero = keep.tile([P, 1], F32, name="zero")
        picked0 = keep.tile([P, PACK, S], F32, name="picked0")
        picked1 = keep.tile([P, PACK * S], F32, name="picked1")
        grouped = [keep.tile([P, S, PACK], BF16, name=f"grouped{a}", align_bytes=256) for a in range(PASSES)]
        codes = [keep.tile([P, S], U32, name=f"codes{a}", align_bytes=256) for a in range(PASSES)]
        scales = [keep.tile([P, S], U8, name=f"scales{a}", align_bytes=256) for a in range(PASSES)]
        result = keep.tile([P, TILES, S], F32, name="result", align_bytes=256)

        quarter_bank = [psum.tile([P, 2, HALF], F32, name=f"quarter{q}") for q in range(2)]
        first_half_bank = {u: psum.tile([P, 2, HALF], F32, name=f"first_half{u}") for u in range(1, PAIRS)}
        second_half_bank = [psum.tile([P, 2, HALF], F32, name=f"second_half{u}") for u in range(LAST_PAIR)]
        second_half_bank.append(quarter_bank[0])
        whole_bank = {t: psum.tile([P, S], F32, name=f"whole{t}") for t in range(SPLIT, TILES)}

        x_view = xT.rearrange("(a p i) t -> a i p t", a=PASSES, i=PACK)
        w_view = w_words.rearrange("a p n -> p a n")
        out_view = out.rearrange("(t p) j -> p t j", p=P)

        def load_plane(n):
            nc.sync.dma_start(planes[n][:], x_view[n // PACK, n % PACK])

        def load_w_scales(a):
            for g in range(4):
                nc.sync.dma_start(
                    ws_sb[32 * g : 32 * g + 4, a, :].bitcast(I32), w_scales[a, 4 * g : 4 * g + 4, :].bitcast(I32)
                )

        def load_w(a, t0, t1):
            cols = slice(2 * P * t0, 2 * P * t1)
            nc.sync.dma_start(w_sb[:, a : a + 1, cols].bitcast(I32), w_view[:, a : a + 1, cols].bitcast(I32))

        nc.vector.memset(b_rows[0 : P // 2, :], 0.0)
        nc.vector.memset(zero[:], 0.0)
        nc.vector.memset(ws_sb[:].rearrange("p a n -> p (a n)").bitcast(I32), 0)
        nc.scalar.activation(b_rows[P // 2 : P, :], zero[P // 2 : P, :].to_broadcast([P // 2, P]), GELU)

        runs = HALF // BLOCK
        nc.sync.dma_start(wg_runs[:], wgt.rearrange("(m r) (J b) -> r m J b", r=REPEAT, b=BLOCK)[0][:, 0:runs, :])
        load_plane(0)
        nc.sync.dma_start(lists[:], offs)
        nc.sync.dma_start(wg[:, HALF:S], wgt[:, HALF:S])
        load_plane(1)
        nc.sync.dma_start(b_rows[0:TILES, :], b.rearrange("(c p) -> c p", p=P))
        for n in range(2, PACK + 1):
            load_plane(n)
        load_w_scales(0)
        load_w(0, 0, EARLY)
        for n in range(PACK + 1, PASSES * PACK):
            load_plane(n)
        load_w(0, EARLY, TILES)
        load_w_scales(1)
        load_w(1, 0, EARLY)
        load_w(1, EARLY, TILES)

        make_identity(nc, ident[:])
        nc.tensor.transpose(whole_bank[TILES - 1][:, 0:P], b_rows[:], ident[:])
        nc.scalar.copy(b_cols[:], whole_bank[TILES - 1][:, 0:TILES])

        nc.vector.transpose(wg_picks[:], wg_runs[:])
        by_run = wg_picks[:].rearrange("p (m J) -> p J m", J=runs)
        rows_in_block = BLOCK // REPEAT
        quarter_runs = QUARTER // BLOCK
        for q in range(2):
            nc.vector.tensor_copy(
                wg_turned[:, q * QUARTER : (q + 1) * QUARTER].rearrange("p (J m r) -> p J m r", m=rows_in_block, r=REPEAT),
                by_run[:, q * quarter_runs : (q + 1) * quarter_runs, :]
                .unsqueeze(3)
                .to_broadcast([P, quarter_runs, rows_in_block, REPEAT]),
            )
        for q in range(2):
            nc.vector.transpose(wg[:, q * QUARTER : (q + 1) * QUARTER], wg_turned[:, q * QUARTER : (q + 1) * QUARTER])

        def gather(n, dst, c0, cn):
            nc.vector.tensor_tensor(
                dst,
                planes[n][:].indirect(lists[:, c0 // LIST_ROWS : (c0 + cn) // LIST_ROWS]),
                wg[:, c0 : c0 + cn],
                MULT,
            )

        def interleave(copy, a, src, c0, cn, i0, i1):
            dst = grouped[a][:, c0 : c0 + cn, i0:i1].rearrange("p (c j) i -> p c i j", j=RUN)
            copy(dst, src.rearrange("p i (c j) -> p c i j", j=RUN))

        def quantize(a, c0, cn):
            nc.vector.quantize_mx(
                out=codes[a][:, c0 : c0 + cn].bitcast(FP8X4),
                scales=scales[a][:, c0 : c0 + cn],
                in_=grouped[a][:, c0 : c0 + cn, :].rearrange("p c i -> p (c i)"),
            )

        def multiply(dst, a, t, c0, cn, first, last):
            nc.tensor.matmul_mx(
                out=dst,
                lhsT=w_sb[:, a, 2 * P * t : 2 * P * (t + 1)].bitcast(FP4X4),
                lhsT_scale=ws_sb[:, a, P * t : P * (t + 1)],
                rhs=codes[a][:, c0 : c0 + cn].bitcast(FP8X4),
                rhs_scale=scales[a][:, c0 : c0 + cn],
                start=first and a == 0,
                stop=last and a == PASSES - 1,
            )

        def multiply_whole(a, t):
            multiply(whole_bank[t][:], a, t, 0, S, True, True)

        def multiply_quarter(a, q):
            for t in range(2):
                multiply(quarter_bank[q][:, t, 0:QUARTER], a, t, q * QUARTER, QUARTER, t == 0, t == 1)

        def multiply_late(bank, a, q):
            for t in range(2):
                multiply(bank[:, t, 0:QUARTER], a, t, q * QUARTER, QUARTER, t == 0, t == 1)

        def multiply_half(bank, a, u, c0):
            if a == 0:
                for s in range(2):
                    multiply(bank[:, s, :], a, 2 * u + s, c0, HALF, s == 0, s == 1)
                return
            for q in range(2):
                for s in range(2):
                    dst = bank[:, s, q * QUARTER : (q + 1) * QUARTER]
                    multiply(dst, a, 2 * u + s, c0 + q * QUARTER, QUARTER, q + s == 0, q + s == 2)

        def finish(src, t, c0, cn):
            nc.scalar.activation(result[:, t, c0 : c0 + cn], src, GELU, bias=b_cols[:, t : t + 1])

        def store(t0, tn, c0, cn):
            nc.sync.dma_start(out_view[:, t0 : t0 + tn, c0 : c0 + cn], result[:, t0 : t0 + tn, c0 : c0 + cn])

        on_scalar, on_vector = nc.scalar.copy, nc.vector.tensor_copy

        gather(0, picked0[:, 0, 0:QUARTER], 0, QUARTER)
        gather(0, picked0[:, 0, QUARTER:S], QUARTER, S - QUARTER)
        gather(1, picked0[:, 1, :], 0, S)
        interleave(on_scalar, 0, picked0[:, 0:2, :], 0, S, 0, 2)
        gather(2, picked0[:, 2, :], 0, S)
        for c0 in (0, HALF):
            gather(3, picked0[:, 3, c0 : c0 + HALF], c0, HALF)
            interleave(on_scalar, 0, picked0[:, 2:4, c0 : c0 + HALF], c0, HALF, 2, 4)

        rows = picked1[:].rearrange("p (i j) -> p i j", i=PACK)
        borrowed6 = S + 3 * QUARTER
        to_borrowed7 = 3 * QUARTER

        def early_pair(q):
            c0 = borrowed6 + q * QUARTER
            return picked1[:, c0 : c0 + 2 * to_borrowed7].rearrange("p (i j) -> p i j", i=2)[:, :, 0:QUARTER]

        gather(4, rows[:, 0, 0 : 3 * QUARTER], 0, 3 * QUARTER)
        quantize(0, 0, HALF)
        gather(4, rows[:, 0, 3 * QUARTER : S], 3 * QUARTER, QUARTER)
        gather(5, rows[:, 1, 0:HALF], 0, HALF)
        interleave(on_scalar, 1, rows[:, 0:2, 0:HALF], 0, HALF, 0, 2)
        quantize(0, HALF, HALF)
        gather(5, rows[:, 1, HALF : 3 * QUARTER], HALF, QUARTER)
        gather(6, picked1[:, borrowed6 : borrowed6 + HALF], 0, HALF)
        for q in range(2):
            multiply_quarter(0, q)
        multiply_half(first_half_bank[1], 0, 1, 0)
        multiply_late(second_half_bank[0], 0, 2)
        multiply_half(second_half_bank[1], 0, 1, HALF)
        multiply_half(first_half_bank[LAST_PAIR], 0, LAST_PAIR, 0)
        for t in whole_bank:
            multiply_whole(0, t)
        for q in range(2):
            gather(7, early_pair(q)[:, 1, :], q * QUARTER, QUARTER)
            interleave(on_scalar, 1, early_pair(q), q * QUARTER, QUARTER, 2, 4)
        gather(7, rows[:, 3, HALF:S], HALF, HALF)
        for c0 in (0, QUARTER):
            quantize(1, c0, QUARTER)
        gather(5, rows[:, 1, 3 * QUARTER : S], 3 * QUARTER, QUARTER)
        for c0 in (HALF, 3 * QUARTER):
            gather(6, rows[:, 2, c0 : c0 + QUARTER], c0, QUARTER)
        for c0 in (HALF, 3 * QUARTER):
            interleave(on_vector, 1, rows[:, :, c0 : c0 + QUARTER], c0, QUARTER, 0, 4)
        for c0 in (HALF, 3 * QUARTER):
            quantize(1, c0, QUARTER)

        for q in range(2):
            multiply_quarter(1, q)
            for t in range(2):
                finish(quarter_bank[q][:, t, 0:QUARTER], t, q * QUARTER, QUARTER)
            store(0, 2, q * QUARTER, QUARTER)
        for u in range(1, PAIRS):
            multiply_half(first_half_bank[u], 1, u, 0)
            for s in range(2):
                finish(first_half_bank[u][:, s, :], 2 * u + s, 0, HALF)
                store(2 * u + s, 1, 0, HALF)
        multiply_late(quarter_bank[1], 0, 3)
        multiply_half(second_half_bank[LAST_PAIR], 0, LAST_PAIR, HALF)

        for q, bank in ((2, second_half_bank[0]), (3, quarter_bank[1])):
            multiply_late(bank, 1, q)
            for t in range(2):
                finish(bank[:, t, 0:QUARTER], t, q * QUARTER, QUARTER)
            store(0, 2, q * QUARTER, QUARTER)
        for u in range(1, LAST_PAIR):
            multiply_half(second_half_bank[u], 1, u, HALF)
            for s in range(2):
                finish(second_half_bank[u][:, s, :], 2 * u + s, HALF, HALF)
                store(2 * u + s, 1, HALF, HALF)
        for t in whole_bank:
            multiply_whole(1, t)
            finish(whole_bank[t][:], t, 0, S)
            store(t, 1, 0, S)
        multiply_half(second_half_bank[LAST_PAIR], 1, LAST_PAIR, HALF)
        finish(second_half_bank[LAST_PAIR][:, 0, :], SPLIT - 2, HALF, HALF)
        store(SPLIT - 2, 1, HALF, HALF)
        finish(second_half_bank[LAST_PAIR][:, 1, :], SPLIT - 1, HALF, HALF)
        nc.scalar.dma_start(out_view[:, SPLIT - 1, HALF:S], result[:, SPLIT - 1, HALF:S])
